import numpy as np
import ml_dtypes


def mxq(x, axis, fmt="e4m3"):
    dtype, down = {"e4m3": (ml_dtypes.float8_e4m3fn, 7), "e5m2": (ml_dtypes.float8_e5m2, 14)}[fmt]
    v = np.moveaxis(np.asarray(x, np.float32).astype(ml_dtypes.bfloat16).astype(np.float64), axis, -1)
    blocks = v.reshape(v.shape[:-1] + (-1, 32))
    amax = np.abs(blocks).max(-1, keepdims=True)
    byte = np.maximum(np.where(amax > 0, np.frexp(amax)[1] - 1 + 127, 0) - down, 1)
    scale = np.exp2(byte - 127.0)
    codes = (blocks / scale).astype(np.float32).astype(dtype).astype(np.float64)
    return np.moveaxis((codes * scale).reshape(v.shape), -1, axis)


WIDE = False


def mx_kscale(k):
    if not WIDE:
        return np.ones(k)
    levels = np.array([10, -10, 5, -5, 0])
    if k % 512:
        return np.exp2(np.random.permutation(np.resize(levels, k // 32))).repeat(32)
    a = np.empty((k // 512, 16))
    for p in range(k // 512):
        a[p, :8] = np.random.permutation(np.resize(levels, 8))
        for g in range(8):
            far = levels[np.abs(levels - a[p, g]) >= 10]
            a[p, g + 8] = far[np.random.randint(len(far))]
    return np.exp2(a.ravel()).repeat(32)


def f64(x):
    return np.asarray(x).astype(np.float64)


def striped(idx):
    return np.tile(idx.reshape(-1, 16).T, (8, 1)).astype(np.uint16)


def unstriped(offs):
    return offs[:16].T.reshape(-1).astype(np.int64)


def pack_weight(w):
    k, n = w.shape
    w = f64(np.asarray(w, np.float32).astype(ml_dtypes.bfloat16)).reshape(k // 32, 32, n)
    amax = np.abs(w).max(1)
    byte = np.clip(np.where(amax > 0, np.frexp(amax)[1] - 1 + 127 - 7, 1), 1, 254)
    scaled = (w * np.exp2(127.0 - byte)[:, None, :]).reshape(k, n).astype(np.float32)
    words = np.ascontiguousarray(scaled.reshape(k // 512, 128, 4, n).transpose(0, 1, 3, 2)).astype(ml_dtypes.float8_e4m3fn).view(np.uint8)
    return words, np.ascontiguousarray(byte.astype(np.uint8).reshape(k // 512, 16, n))


def unpack_weight(words, scales):
    g, p, n, _ = words.shape
    vals = np.ascontiguousarray(words).view(ml_dtypes.float8_e4m3fn).astype(np.float64) * np.repeat(np.exp2(scales.astype(np.float64) - 127.0), 8, axis=1)[..., None]
    return vals.transpose(0, 1, 3, 2).reshape(g * 512, n)


E2M1 = np.array([0.0, 0.5, 1.0, 1.5, 2.0, 3.0, 4.0, 6.0, -0.0, -0.5, -1.0, -1.5, -2.0, -3.0, -4.0, -6.0])


def pack_fp4(w):
    k, n = w.shape
    w = f64(np.asarray(w, np.float32).astype(ml_dtypes.bfloat16)).reshape(k // 32, 32, n)
    amax = np.abs(w).max(1)
    mant, ex = np.frexp(amax / 6.0)
    byte = np.clip(np.where(amax > 0, np.where(mant > 0.5, ex, ex - 1) + 127, 1), 1, 254)
    scaled = (w * np.exp2(127.0 - byte)[:, None, :]).reshape(k, n).astype(np.float32)
    c = np.ascontiguousarray(scaled.reshape(k // 512, 128, 4, n).transpose(0, 1, 3, 2)).astype(ml_dtypes.float4_e2m1fn).view(np.uint8) & 0xF
    words = (c[..., 0::2] | (c[..., 1::2] << 4)).reshape(k // 512, 128, 2 * n)
    return np.ascontiguousarray(words), np.ascontiguousarray(byte.astype(np.uint8).reshape(k // 512, 16, n))


def unpack_fp4(words, scales):
    g, _, n = scales.shape
    words = np.ascontiguousarray(words).reshape(g, 128, n, 2)
    nib = np.empty((g, 128, n, 4), np.uint8)
    nib[..., 0::2] = words & 0xF
    nib[..., 1::2] = words >> 4
    vals = E2M1[nib] * np.repeat(np.exp2(scales.astype(np.float64) - 127.0), 8, axis=1)[..., None]
    return vals.transpose(0, 1, 3, 2).reshape(g * 512, n)


def sigmoid(v):
    return 1.0 / (1.0 + np.exp(-np.maximum(v, -700.0)))

def planes(y):
    n, m = y.shape
    v = y.astype(np.float32).astype(ml_dtypes.bfloat16).astype(np.float64).reshape(n // 32, 32, m)
    top = np.abs(v).max(1)
    byte = np.clip(np.where(top > 0, np.frexp(top)[1] - 1 + 127 - 7, 1), 1, 254)
    codes = (v * np.exp2(127.0 - byte)[:, None, :]).reshape(n, m).astype(np.float32).astype(ml_dtypes.float8_e4m3fn).view(np.uint8)
    words = codes.reshape(n // 512, 128, 4, m).transpose(0, 1, 3, 2)
    return np.ascontiguousarray(words), np.ascontiguousarray(byte.astype(np.uint8).reshape(n // 512, 16, m))


K, T, S, N, H, W = 512, 2048, 512, 512, 512, 2048


def setup_inputs():
    n = np.random.standard_normal
    s = mx_kscale(K)[:, None]
    u = mx_kscale(H)
    packed_xT = pack_weight(n((K, T)) * s)
    packed_w1 = pack_fp4(n((K, H)) / np.sqrt(K) / s)
    packed_w2 = pack_fp4(n((H, N)) / np.sqrt(2 * H) / u[:, None])
    packed_w3 = pack_fp4(n((K, N)) / np.sqrt(2 * K) / s)
    return {
        "x_words": packed_xT[0],
        "x_scales": packed_xT[1],
        "w1_words": packed_w1[0],
        "w1_scales": packed_w1[1],
        "gn": (np.random.uniform(0.5, 1.5, (H, 1)) * u[:, None]).astype(np.float32),
        "w2_words": packed_w2[0],
        "w2_scales": packed_w2[1],
        "w3_words": packed_w3[0],
        "w3_scales": packed_w3[1],
        "offs": striped(np.random.permutation(T)[:S]),
        "n1": striped(np.random.permutation(S)),
        "n2": striped(np.random.permutation(S)),
        "two": striped(np.random.permutation(T)[:S]),
        "n3": striped(np.random.randint(0, S, W)),
    }


def reference(x_words, x_scales, w1_words, w1_scales, gn, w2_words, w2_scales, w3_words, w3_scales, offs, n1, n2, two, n3):
    xq = unpack_weight(x_words, x_scales)[:, unstriped(offs)]
    y = unpack_fp4(w1_words, w1_scales).T @ xq
    st = y * (sigmoid(y[:, unstriped(n1)]))
    z = f64(gn) * (st - st[:, unstriped(n2)])
    x_two = unpack_weight(x_words, x_scales)[:, unstriped(two)]
    h = unpack_fp4(w2_words, w2_scales).T @ mxq(z, 0, "e4m3") + unpack_fp4(w3_words, w3_scales).T @ x_two
    mb = h[:, unstriped(n3)]
    mx = mb.reshape(N, S, 4).max(axis=2)
    mn = mb.reshape(N, S, 4).min(axis=2)
    out_0 = mx * np.tanh(h - mn)
    return (out_0,) + planes(out_0)

@@ -1,0 +1,239 @@
+from contextlib import ExitStack
+
+import concourse.mybir as mybir
+
+K, T, S, N, H = 512, 2048, 512, 512, 512
+FLOPS = 3 * 2 * 512 * 512 * 512
+
+F32 = mybir.dt.float32
+BF16 = mybir.dt.bfloat16
+I32 = mybir.dt.int32
+U32 = mybir.dt.uint32
+U16 = mybir.dt.uint16
+U8 = mybir.dt.uint8
+FP8X4 = mybir.dt.float8_e4m3fn_x4
+FP4X4 = mybir.dt.float4_e2m1fn_x4
+ALU = mybir.AluOpType
+ACT = mybir.ActivationFunctionType
+
+P = 128
+PACK = 4
+HALF = S // 2
+SIG_W = 704
+H_W = 544
+Z_PIECES = (256, 256)
+CHUNKS = (128, 128, 128, 64, 64)
+N1_ON_VECTOR = (0,)
+N2_ON_VECTOR = ((1, 3),)
+N3_ON_VECTOR = ((0, 1),)
+H_ON_SCALAR = (0,)
+CAST_ON_VECTOR = (0, 1, 2, 3)
+
+
+def tile_picked_mixinhopggtan_none_po_kernel(
+    tc, x_words, x_scales, w1_words, w1_scales, gn, w2_words, w2_scales, w3_words, w3_scales,
+    offs, n1, n2, two, n3, out_0, out_1, out_2,
+):
+    nc = tc.nc
+    with ExitStack() as ctx:
+        keep = ctx.enter_context(tc.tile_pool(name="keep", bufs=1))
+        ring = ctx.enter_context(tc.tile_pool(name="ring", bufs=2))
+        work = ctx.enter_context(tc.tile_pool(name="work", bufs=3))
+        psum = ctx.enter_context(tc.psum_pool(name="psum", bufs=1))
+
+        def gather(on_vector, out, window, offsets):
+            if on_vector:
+                nc.vector.tensor_copy(out=out, in_=window.indirect(offsets))
+            else:
+                nc.scalar.activation(out=out, in_=window.indirect(offsets), func=ACT.Copy)
+
+        def load_list(name, src):
+            t = keep.tile(list(src.shape), U16, name=name)
+            nc.sync.dma_start(out=t[:], in_=src)
+            return t
+
+        def load_scale_rows(dst, src, eng):
+            for q in range(4):
+                eng.dma_start(
+                    out=dst[32 * q : 32 * q + 4, :].bitcast(I32), in_=src[0, 4 * q : 4 * q + 4, :].bitcast(I32)
+                )
+
+        def load_weight_words(src, eng):
+            t = keep.tile([P, 2 * N], U8, name="w_raw")
+            eng.dma_start(out=t[:].bitcast(I32), in_=src[0].bitcast(I32))
+            return t
+
+        def deal_words(name, raw, eng):
+            t = keep.tile([P, PACK, P, 2], U8, name=name, align_bytes=64)
+            eng.tensor_copy(out=t[:], in_=raw.rearrange("p (m t b) -> p t m b", t=PACK, b=2))
+            return t
+
+        def deal_scales(name, raw):
+            t = keep.tile([P, PACK, P], U8, name=name, align_bytes=64)
+            nc.vector.tensor_copy(out=t[:], in_=raw.rearrange("p (m t) -> p t m", t=PACK))
+            return t
+
+        def product(out, w, ws, t, codes, scales, start, stop):
+            nc.tensor.matmul_mx(
+                out=out,
+                lhsT=w[:, t].rearrange("p m b -> p (m b)").bitcast(FP4X4),
+                lhsT_scale=ws[:, t, :],
+                rhs=codes.bitcast(FP8X4),
+                rhs_scale=scales,
+                start=start,
+                stop=stop,
+            )
+
+        ws_raw = keep.tile([P, 2 * N], U8, name="ws_raw")
+        nc.gpsimd.memset(ws_raw[:].bitcast(I32), 0)
+        xs = keep.tile([P, T], U8, name="xs")
+        nc.gpsimd.memset(xs[:].bitcast(I32), 0)
+
+        offs_sb = load_list("offs_sb", offs)
+        w1_raw = load_weight_words(w1_words, nc.sync)
+        load_scale_rows(ws_raw[:, N // 2 : N // 2 + N], w1_scales, nc.sync)
+        load_scale_rows(xs, x_scales, nc.sync)
+        xw = keep.tile([P, T], U32, name="xw")
+        nc.sync.dma_start(out=xw[:].bitcast(I32), in_=x_words[0].rearrange("p n t -> p (n t)").bitcast(I32))
+        two_sb = load_list("two_sb", two)
+        n1_sb = load_list("n1_sb", n1)
+        gain = keep.tile([P, PACK], F32, name="gain")
+        nc.gpsimd.dma_start(out=gain[:], in_=gn.rearrange("(p t) o -> p (t o)", t=PACK))
+        n2_sb = load_list("n2_sb", n2)
+        n3_sb = load_list("n3_sb", n3)
+
+        sig = [keep.tile([P, SIG_W], F32, name="sig%d" % t) for t in range(PACK)]
+        hwin = [keep.tile([P, H_W], F32, name="hwin%d" % t) for t in range(PACK)]
+        for t in range(PACK):
+            nc.gpsimd.memset(sig[t][:, S:], 0.0)
+            nc.gpsimd.memset(hwin[t][:, S:], 0.0)
+
+        w1 = deal_words("w1", w1_raw[:], nc.vector)
+        w1s = deal_scales("w1s", ws_raw[:, N // 2 : N // 2 + N])
+        x1s = keep.tile([P, S], U8, name="picked_scales", align_bytes=64)
+        nc.vector.tensor_copy(out=x1s[:], in_=xs[:].indirect(offs_sb[:]))
+        y = [psum.tile([P, S], F32, name="y%d" % t) for t in range(PACK)]
+        x1w = [keep.tile([P, HALF], U32, name="picked_words%d" % u, align_bytes=64) for u in range(2)]
+        for u in range(2):
+            cols = slice(u * HALF, (u + 1) * HALF)
+            nc.vector.tensor_copy(out=x1w[u][:], in_=xw[:].indirect(offs_sb[:, u * 16 : (u + 1) * 16]))
+            for t in range(PACK):
+                product(y[t][:, cols], w1, w1s, t, x1w[u][:], x1s[:, cols], True, True)
+
+        for t in range(PACK):
+            nc.scalar.activation(out=sig[t][:, :S], in_=y[t][:], func=ACT.Sigmoid)
+
+        x2w = [keep.tile([P, HALF], U32, name="picked_words%d" % u, align_bytes=64) for u in range(2)]
+        for u in range(2):
+            nc.vector.tensor_copy(out=x2w[u][:], in_=xw[:].indirect(two_sb[:, u * 16 : (u + 1) * 16]))
+        x2s = keep.tile([P, S], U8, name="picked_scales", align_bytes=64)
+        nc.vector.tensor_copy(out=x2s[:], in_=xs[:].indirect(two_sb[:]))
+
+        st = keep.tile([P, PACK, S], F32, name="st")
+        sg = [keep.tile([P, S], F32, name="sg%d" % t) for t in range(PACK)]
+        for t in range(PACK):
+            gather(t in N1_ON_VECTOR, sg[t][:], sig[t][:], n1_sb[:])
+            nc.vector.scalar_tensor_tensor(
+                out=st[:, t, :], in0=y[t][:], scalar=gain[:, t : t + 1], in1=sg[t][:], op0=ALU.mult, op1=ALU.mult
+            )
+
+        w_late = keep.tile([P, 2, 2 * N], U8, name="w_raw")
+        nc.sync.dma_start(out=w_late[:, 0, :].bitcast(I32), in_=w3_words[0].bitcast(I32))
+        load_scale_rows(ws_raw[:, :N], w3_scales, nc.sync)
+        nc.sync.dma_start(out=w_late[:, 1, :].bitcast(I32), in_=w2_words[0].bitcast(I32))
+        load_scale_rows(ws_raw[:, N:], w2_scales, nc.sync)
+        w3 = deal_words("w3", w_late[:, 0, :], nc.vector)
+        w3s = deal_scales("w3s", ws_raw[:, :N])
+        w2 = deal_words("w2", w_late[:, 1, :], nc.vector)
+        w2s = deal_scales("w2s", ws_raw[:, N:])
+        h = [psum.tile([P, S], F32, name="h%d" % t) for t in range(PACK)]
+        for u in range(2):
+            cols = slice(u * HALF, (u + 1) * HALF)
+            for t in range(PACK):
+                product(h[t][:, cols], w3, w3s, t, x2w[u][:], x2s[:, cols], u == 0, False)
+
+        c0 = 0
+        for u, w in enumerate(Z_PIECES):
+            cols = slice(c0, c0 + w)
+            st2 = keep.tile([P, PACK, w], F32, name="st2_%d" % u)
+            for t in range(PACK):
+                gather((u, t) in N2_ON_VECTOR, st2[:, t, :], st[:, t, :], n2_sb[:, c0 // 16 : (c0 + w) // 16])
+            zb = keep.tile([P, w, PACK], BF16, name="zb%d" % u, align_bytes=64)
+            nc.vector.tensor_tensor(
+                out=zb[:].rearrange("p (c i) t -> p c t i", i=4),
+                in0=st[:, :, cols].rearrange("p t (c i) -> p c t i", i=4),
+                in1=st2[:].rearrange("p t (c i) -> p c t i", i=4),
+                op=ALU.subtract,
+            )
+            zw = keep.tile([P, w], U32, name="zw%d" % u, align_bytes=64)
+            zs = keep.tile([P, w], U8, name="zs%d" % u, align_bytes=64)
+            nc.vector.quantize_mx(out=zw[:].bitcast(FP8X4), scales=zs[:], in_=zb[:].rearrange("p c t -> p (c t)"))
+            for t in range(PACK):
+                product(h[t][:, cols], w2, w2s, t, zw[:], zs[:], False, u == len(Z_PIECES) - 1)
+            c0 = c0 + w
+
+        hall = keep.tile([P, PACK, S], F32, name="hall")
+        for t in range(PACK):
+            if t in H_ON_SCALAR:
+                nc.scalar.copy(out=hwin[t][:, :S], in_=h[t][:])
+            else:
+                nc.vector.tensor_copy(out=hwin[t][:, :S], in_=h[t][:])
+            nc.sync.dma_start(out=hall[:, t, :], in_=hwin[t][:, :S])
+
+        ow = keep.tile([P, S], U32, name="ow", align_bytes=64)
+        osc = keep.tile([P, S], U8, name="osc", align_bytes=64)
+        out_rows = out_0.rearrange("(p t) c -> p t c", t=PACK)
+        out_words = out_1[0].rearrange("p c r -> p (c r)").bitcast(I32)
+
+        def finish(c, c0, w, top, th):
+            cols = slice(c0, c0 + w)
+            o = work.tile([P, PACK, w], F32, name="o")
+            nc.vector.tensor_tensor(out=o[:], in0=top[:], in1=th[:], op=ALU.mult)
+            nc.sync.dma_start(out=out_rows[:, :, cols], in_=o[:])
+            ob = work.tile([P, w, PACK], BF16, name="ob", align_bytes=64)
+            dst = ob[:].rearrange("p (c i) t -> p c t i", i=4)
+            src = o[:].rearrange("p t (c i) -> p c t i", i=4)
+            if c in CAST_ON_VECTOR:
+                nc.vector.tensor_copy(out=dst, in_=src)
+            else:
+                nc.scalar.copy(out=dst, in_=src)
+            nc.vector.quantize_mx(
+                out=ow[:, cols].bitcast(FP8X4), scales=osc[:, cols], in_=ob[:].rearrange("p c t -> p (c t)")
+            )
+            nc.sync.dma_start(out=out_words[:, cols], in_=ow[:, cols].bitcast(I32))
+
+        c0 = 0
+        pending = None
+        for c, w in enumerate(CHUNKS):
+            cols = slice(c0, c0 + w)
+            mb = ring.tile([P, PACK, 4 * w], F32, name="mb")
+            for t in range(PACK):
+                gather((c, t) in N3_ON_VECTOR, mb[:, t, :], hwin[t][:], n3_sb[:, c0 // 4 : (c0 + w) // 4])
+            members = mb[:].rearrange("p t (j m) -> p (t j) m", m=4)
+            lo2 = work.tile([P, PACK * w, 2], F32, name="lo2")
+            hi2 = work.tile([P, PACK * w, 2], F32, name="hi2")
+            nc.vector.tensor_tensor(out=lo2[:], in0=members[:, :, 0:2], in1=members[:, :, 2:4], op=ALU.min)
+            nc.vector.tensor_tensor(out=hi2[:], in0=members[:, :, 0:2], in1=members[:, :, 2:4], op=ALU.max)
+            lo = work.tile([P, PACK, w], F32, name="lo")
+            nc.vector.tensor_tensor(
+                out=lo[:].rearrange("p t j -> p (t j)"), in0=lo2[:, :, 0], in1=lo2[:, :, 1], op=ALU.min
+            )
+            top = work.tile([P, PACK, w], F32, name="top")
+            nc.vector.tensor_tensor(
+                out=top[:].rearrange("p t j -> p (t j)"), in0=hi2[:, :, 0], in1=hi2[:, :, 1], op=ALU.max
+            )
+            d = work.tile([P, PACK, w], F32, name="d")
+            nc.vector.tensor_tensor(out=d[:], in0=hall[:, :, cols], in1=lo[:], op=ALU.subtract)
+            th = work.tile([P, PACK, w], F32, name="th")
+            nc.scalar.activation(out=th[:], in_=d[:], func=ACT.Tanh)
+            if pending is not None:
+                finish(*pending)
+            pending = (c, c0, w, top, th)
+            c0 = c0 + w
+        finish(*pending)
+
+        for q in range(4):
+            eng = nc.scalar if q % 2 == 0 else nc.sync
+            eng.dma_start(
+                out=out_2[0, 4 * q : 4 * q + 4, :].bitcast(I32), in_=osc[32 * q : 32 * q + 4, :].bitcast(I32)
+            )

@@ -1,6 +1,7 @@
 from contextlib import ExitStack
 
 import concourse.mybir as mybir
+from concourse.masks import make_identity
 
 K, T, S, N, H = 512, 2048, 512, 512, 512
 FLOPS = 3 * 2 * 512 * 512 * 512
@@ -21,13 +22,14 @@ PACK = 4
 HALF = S // 2
 SIG_W = 704
 H_W = 544
-Z_PIECES = (256, 256)
-CHUNKS = (128, 128, 128, 64, 64)
+Z_PIECES = (256, 128, 128)
+CHUNKS = (64, 128, 128, 128, 64)
+LAG = 1
 N1_ON_VECTOR = (0,)
-N2_ON_VECTOR = ((1, 3),)
-N3_ON_VECTOR = ((0, 1),)
+N2_ON_VECTOR = ((0, 3), (1, 3))
+N3_ON_VECTOR = ((0, 2), (0, 3), (1, 3), (2, 3))
 H_ON_SCALAR = (0,)
-CAST_ON_VECTOR = (0, 1, 2, 3)
+CAST_ON_VECTOR = (0, 1)
 
 
 def tile_picked_mixinhopggtan_none_po_kernel(
@@ -41,27 +43,26 @@ def tile_picked_mixinhopggtan_none_po_kernel(
         work = ctx.enter_context(tc.tile_pool(name="work", bufs=3))
         psum = ctx.enter_context(tc.psum_pool(name="psum", bufs=1))
 
-        def gather(on_vector, out, window, offsets):
-            if on_vector:
+        def gather(on_vector, out, window, offsets, sign=1.0):
+            if on_vector and sign < 0:
+                nc.vector.tensor_scalar(
+                    out=out, in0=window.indirect(offsets), scalar1=sign, scalar2=0.0, op0=ALU.mult, op1=ALU.add
+                )
+            elif on_vector:
                 nc.vector.tensor_copy(out=out, in_=window.indirect(offsets))
             else:
-                nc.scalar.activation(out=out, in_=window.indirect(offsets), func=ACT.Copy)
+                nc.scalar.activation(out=out, in_=window.indirect(offsets), func=ACT.Copy, scale=sign)
 
         def load_list(name, src):
             t = keep.tile(list(src.shape), U16, name=name)
             nc.sync.dma_start(out=t[:], in_=src)
             return t
 
-        def load_scale_rows(dst, src, eng):
+        def load_scale_rows(dst, src, queues):
             for q in range(4):
-                eng.dma_start(
+                queues[q].dma_start(
                     out=dst[32 * q : 32 * q + 4, :].bitcast(I32), in_=src[0, 4 * q : 4 * q + 4, :].bitcast(I32)
                 )
-
-        def load_weight_words(src, eng):
-            t = keep.tile([P, 2 * N], U8, name="w_raw")
-            eng.dma_start(out=t[:].bitcast(I32), in_=src[0].bitcast(I32))
-            return t
 
         def deal_words(name, raw, eng):
             t = keep.tile([P, PACK, P, 2], U8, name=name, align_bytes=64)
@@ -84,17 +85,20 @@ def tile_picked_mixinhopggtan_none_po_kernel(
                 stop=stop,
             )
 
-        ws_raw = keep.tile([P, 2 * N], U8, name="ws_raw")
-        nc.gpsimd.memset(ws_raw[:].bitcast(I32), 0)
+        on_sync = [nc.sync] * 4
         xs = keep.tile([P, T], U8, name="xs")
-        nc.gpsimd.memset(xs[:].bitcast(I32), 0)
+        nc.vector.memset(xs[:].bitcast(I32), 0)
+        ws_raw = keep.tile([P, 2 * N], U8, name="ws_raw")
+        nc.vector.memset(ws_raw[:].bitcast(I32), 0)
 
         offs_sb = load_list("offs_sb", offs)
-        w1_raw = load_weight_words(w1_words, nc.sync)
-        load_scale_rows(ws_raw[:, N // 2 : N // 2 + N], w1_scales, nc.sync)
-        load_scale_rows(xs, x_scales, nc.sync)
+        w1_raw = keep.tile([P, 2 * N], U8, name="w_raw")
+        nc.sync.dma_start(out=w1_raw[:].bitcast(I32), in_=w1_words[0].bitcast(I32))
+        load_scale_rows(xs, x_scales, on_sync)
         xw = keep.tile([P, T], U32, name="xw")
         nc.sync.dma_start(out=xw[:].bitcast(I32), in_=x_words[0].rearrange("p n t -> p (n t)").bitcast(I32))
+        w1s_raw = ws_raw[:, N // 2 : N // 2 + N]
+        load_scale_rows(w1s_raw, w1_scales, on_sync)
         two_sb = load_list("two_sb", two)
         n1_sb = load_list("n1_sb", n1)
         gain = keep.tile([P, PACK], F32, name="gain")
@@ -102,32 +106,30 @@ def tile_picked_mixinhopggtan_none_po_kernel(
         n2_sb = load_list("n2_sb", n2)
         n3_sb = load_list("n3_sb", n3)
 
-        sig = [keep.tile([P, SIG_W], F32, name="sig%d" % t) for t in range(PACK)]
-        hwin = [keep.tile([P, H_W], F32, name="hwin%d" % t) for t in range(PACK)]
+        sig = [keep.tile([P, SIG_W if t in N1_ON_VECTOR else H_W], F32, name="sig%d" % t) for t in range(PACK)]
+        hwin = [keep.tile([P, 2048 if t == 3 else H_W], F32, name="hwin%d" % t) for t in range(PACK)]
         for t in range(PACK):
             nc.gpsimd.memset(sig[t][:, S:], 0.0)
             nc.gpsimd.memset(hwin[t][:, S:], 0.0)
+        ident = keep.tile([P, P], F32, name="ident")
+        make_identity(nc, ident[:])
 
         w1 = deal_words("w1", w1_raw[:], nc.vector)
-        w1s = deal_scales("w1s", ws_raw[:, N // 2 : N // 2 + N])
+        w1s = deal_scales("w1s", w1s_raw)
         x1s = keep.tile([P, S], U8, name="picked_scales", align_bytes=64)
         nc.vector.tensor_copy(out=x1s[:], in_=xs[:].indirect(offs_sb[:]))
-        y = [psum.tile([P, S], F32, name="y%d" % t) for t in range(PACK)]
+        y = [psum.tile([P, S], F32, name="bank%d" % t) for t in range(PACK)]
         x1w = [keep.tile([P, HALF], U32, name="picked_words%d" % u, align_bytes=64) for u in range(2)]
         for u in range(2):
             cols = slice(u * HALF, (u + 1) * HALF)
             nc.vector.tensor_copy(out=x1w[u][:], in_=xw[:].indirect(offs_sb[:, u * 16 : (u + 1) * 16]))
-            for t in range(PACK):
+        for t in range(PACK):
+            for u in range(2):
+                cols = slice(u * HALF, (u + 1) * HALF)
                 product(y[t][:, cols], w1, w1s, t, x1w[u][:], x1s[:, cols], True, True)
 
         for t in range(PACK):
             nc.scalar.activation(out=sig[t][:, :S], in_=y[t][:], func=ACT.Sigmoid)
-
-        x2w = [keep.tile([P, HALF], U32, name="picked_words%d" % u, align_bytes=64) for u in range(2)]
-        for u in range(2):
-            nc.vector.tensor_copy(out=x2w[u][:], in_=xw[:].indirect(two_sb[:, u * 16 : (u + 1) * 16]))
-        x2s = keep.tile([P, S], U8, name="picked_scales", align_bytes=64)
-        nc.vector.tensor_copy(out=x2s[:], in_=xs[:].indirect(two_sb[:]))
 
         st = keep.tile([P, PACK, S], F32, name="st")
         sg = [keep.tile([P, S], F32, name="sg%d" % t) for t in range(PACK)]
@@ -137,11 +139,17 @@ def tile_picked_mixinhopggtan_none_po_kernel(
                 out=st[:, t, :], in0=y[t][:], scalar=gain[:, t : t + 1], in1=sg[t][:], op0=ALU.mult, op1=ALU.mult
             )
 
+        x2w = [keep.tile([P, HALF], U32, name="picked_words%d" % u, align_bytes=64) for u in range(2)]
+        for u in range(2):
+            nc.vector.tensor_copy(out=x2w[u][:], in_=xw[:].indirect(two_sb[:, u * 16 : (u + 1) * 16]))
+        x2s = keep.tile([P, S], U8, name="x2s", align_bytes=64)
+        nc.vector.tensor_copy(out=x2s[:], in_=xs[:].indirect(two_sb[:]))
+
         w_late = keep.tile([P, 2, 2 * N], U8, name="w_raw")
         nc.sync.dma_start(out=w_late[:, 0, :].bitcast(I32), in_=w3_words[0].bitcast(I32))
-        load_scale_rows(ws_raw[:, :N], w3_scales, nc.sync)
+        load_scale_rows(ws_raw[:, :N], w3_scales, on_sync)
         nc.sync.dma_start(out=w_late[:, 1, :].bitcast(I32), in_=w2_words[0].bitcast(I32))
-        load_scale_rows(ws_raw[:, N:], w2_scales, nc.sync)
+        load_scale_rows(ws_raw[:, N:], w2_scales, on_sync)
         w3 = deal_words("w3", w_late[:, 0, :], nc.vector)
         w3s = deal_scales("w3s", ws_raw[:, :N])
         w2 = deal_words("w2", w_late[:, 1, :], nc.vector)
@@ -152,17 +160,20 @@ def tile_picked_mixinhopggtan_none_po_kernel(
             for t in range(PACK):
                 product(h[t][:, cols], w3, w3s, t, x2w[u][:], x2s[:, cols], u == 0, False)
 
+        early = keep.tile([P, PACK * HALF], F32, name="early")
+        late = keep.tile([P, PACK * HALF], F32, name="sg3")
         c0 = 0
         for u, w in enumerate(Z_PIECES):
             cols = slice(c0, c0 + w)
-            st2 = keep.tile([P, PACK, w], F32, name="st2_%d" % u)
+            st2 = early if c0 < HALF else late
+            st2 = st2[:, PACK * (c0 % HALF) : PACK * (c0 % HALF + w)].rearrange("p (t c) -> p t c", t=PACK)
             for t in range(PACK):
                 gather((u, t) in N2_ON_VECTOR, st2[:, t, :], st[:, t, :], n2_sb[:, c0 // 16 : (c0 + w) // 16])
             zb = keep.tile([P, w, PACK], BF16, name="zb%d" % u, align_bytes=64)
             nc.vector.tensor_tensor(
                 out=zb[:].rearrange("p (c i) t -> p c t i", i=4),
                 in0=st[:, :, cols].rearrange("p t (c i) -> p c t i", i=4),
-                in1=st2[:].rearrange("p t (c i) -> p c t i", i=4),
+                in1=st2.rearrange("p t (c i) -> p c t i", i=4),
                 op=ALU.subtract,
             )
             zw = keep.tile([P, w], U32, name="zw%d" % u, align_bytes=64)
@@ -172,23 +183,21 @@ def tile_picked_mixinhopggtan_none_po_kernel(
                 product(h[t][:, cols], w2, w2s, t, zw[:], zs[:], False, u == len(Z_PIECES) - 1)
             c0 = c0 + w
 
-        hall = keep.tile([P, PACK, S], F32, name="hall")
         for t in range(PACK):
             if t in H_ON_SCALAR:
                 nc.scalar.copy(out=hwin[t][:, :S], in_=h[t][:])
             else:
                 nc.vector.tensor_copy(out=hwin[t][:, :S], in_=h[t][:])
-            nc.sync.dma_start(out=hall[:, t, :], in_=hwin[t][:, :S])
 
         ow = keep.tile([P, S], U32, name="ow", align_bytes=64)
         osc = keep.tile([P, S], U8, name="osc", align_bytes=64)
         out_rows = out_0.rearrange("(p t) c -> p t c", t=PACK)
         out_words = out_1[0].rearrange("p c r -> p (c r)").bitcast(I32)
 
-        def finish(c, c0, w, top, th):
+        def finish(c, c0, w, factor, th):
             cols = slice(c0, c0 + w)
             o = work.tile([P, PACK, w], F32, name="o")
-            nc.vector.tensor_tensor(out=o[:], in0=top[:], in1=th[:], op=ALU.mult)
+            nc.vector.tensor_tensor(out=o[:], in0=factor[:], in1=th[:], op=ALU.mult)
             nc.sync.dma_start(out=out_rows[:, :, cols], in_=o[:])
             ob = work.tile([P, w, PACK], BF16, name="ob", align_bytes=64)
             dst = ob[:].rearrange("p (c i) t -> p c t i", i=4)
@@ -203,34 +212,53 @@ def tile_picked_mixinhopggtan_none_po_kernel(
             nc.sync.dma_start(out=out_words[:, cols], in_=ow[:, cols].bitcast(I32))
 
         c0 = 0
-        pending = None
+        pending = []
         for c, w in enumerate(CHUNKS):
             cols = slice(c0, c0 + w)
+            on_tensor = w == P
+            sign = -1.0 if on_tensor else 1.0
+            inner_op, factor_op = (ALU.max, ALU.min) if on_tensor else (ALU.min, ALU.max)
             mb = ring.tile([P, PACK, 4 * w], F32, name="mb")
             for t in range(PACK):
-                gather((c, t) in N3_ON_VECTOR, mb[:, t, :], hwin[t][:], n3_sb[:, c0 // 4 : (c0 + w) // 4])
+                gather((c, t) in N3_ON_VECTOR, mb[:, t, :], hwin[t][:], n3_sb[:, c0 // 4 : (c0 + w) // 4], sign)
             members = mb[:].rearrange("p t (j m) -> p (t j) m", m=4)
-            lo2 = work.tile([P, PACK * w, 2], F32, name="lo2")
-            hi2 = work.tile([P, PACK * w, 2], F32, name="hi2")
-            nc.vector.tensor_tensor(out=lo2[:], in0=members[:, :, 0:2], in1=members[:, :, 2:4], op=ALU.min)
-            nc.vector.tensor_tensor(out=hi2[:], in0=members[:, :, 0:2], in1=members[:, :, 2:4], op=ALU.max)
-            lo = work.tile([P, PACK, w], F32, name="lo")
-            nc.vector.tensor_tensor(
-                out=lo[:].rearrange("p t j -> p (t j)"), in0=lo2[:, :, 0], in1=lo2[:, :, 1], op=ALU.min
-            )
-            top = work.tile([P, PACK, w], F32, name="top")
-            nc.vector.tensor_tensor(
-                out=top[:].rearrange("p t j -> p (t j)"), in0=hi2[:, :, 0], in1=hi2[:, :, 1], op=ALU.max
-            )
-            d = work.tile([P, PACK, w], F32, name="d")
-            nc.vector.tensor_tensor(out=d[:], in0=hall[:, :, cols], in1=lo[:], op=ALU.subtract)
-            th = work.tile([P, PACK, w], F32, name="th")
-            nc.scalar.activation(out=th[:], in_=d[:], func=ACT.Tanh)
-            if pending is not None:
-                finish(*pending)
-            pending = (c, c0, w, top, th)
+            inner2 = work.tile([P, PACK * w, 2], F32, name="inner2")
+            factor2 = work.tile([P, PACK * w, 2], F32, name="factor2")
+            factor = work.tile([P, PACK, w], F32, name="factor")
+            spent = mb[:, 0, :].rearrange("p (t j) -> p t j", t=PACK)
+            inner = spent if on_tensor else work.tile([P, PACK, w], F32, name="inner")[:]
+            steps = [(inner2, inner, inner_op), (factor2, factor[:], factor_op)]
+            if on_tensor:
+                steps = steps[::-1]
+            for pairs, whole, op in steps:
+                nc.vector.tensor_tensor(out=pairs[:], in0=members[:, :, 0:2], in1=members[:, :, 2:4], op=op)
+            for pairs, whole, op in steps:
+                nc.vector.tensor_tensor(
+                    out=whole.rearrange("p t j -> p (t j)"), in0=pairs[:, :, 0], in1=pairs[:, :, 1], op=op
+                )
+            if on_tensor:
+                d_t = psum.tile([P, PACK, P], F32, name="bank%d" % (c % 2))
+                for t in range(PACK):
+                    nc.tensor.matmul(d_t[:, t, :], hwin[t][:, cols], ident[:], start=True, stop=False, is_transpose=True)
+                    nc.tensor.matmul(d_t[:, t, :], inner[:, t, :], ident[:], start=False, stop=True, is_transpose=True)
+                th_t = work.tile([P, PACK, P], F32, name="th_t")
+                nc.scalar.activation(out=th_t[:], in_=d_t[:], func=ACT.Tanh, scale=-1.0)
+                th = psum.tile([P, PACK, P], F32, name="bank%d" % (2 + c % 2))
+                for t in range(PACK):
+                    nc.tensor.transpose(th[:, t, :], th_t[:, t, :], ident[:])
+            else:
+                d = spent
+                for t in range(PACK):
+                    nc.vector.tensor_tensor(out=d[:, t, :], in0=h[t][:, cols], in1=inner[:, t, :], op=ALU.subtract)
+                th = work.tile([P, PACK, w], F32, name="th")
+                nc.scalar.activation(out=th[:], in_=d, func=ACT.Tanh)
+            pending.append((c, c0, w, factor, th))
+            if len(pending) > LAG:
+                finish(*pending[0])
+                pending = pending[1:]
             c0 = c0 + w
-        finish(*pending)
+        for rest in pending:
+            finish(*rest)
 
         for q in range(4):
             eng = nc.scalar if q % 2 == 0 else nc.sync

@@ -24,12 +24,12 @@ SIG_W = 704
 H_W = 544
 Z_PIECES = (256, 128, 128)
 CHUNKS = (64, 128, 128, 128, 64)
-LAG = 1
+LAG = 2
 N1_ON_VECTOR = (0,)
 N2_ON_VECTOR = ((0, 3), (1, 3))
 N3_ON_VECTOR = ((0, 2), (0, 3), (1, 3), (2, 3))
 H_ON_SCALAR = (0,)
-CAST_ON_VECTOR = (0, 1)
+CAST_ON_VECTOR = (0,)
 
 
 def tile_picked_mixinhopggtan_none_po_kernel(
@@ -39,7 +39,7 @@ def tile_picked_mixinhopggtan_none_po_kernel(
     nc = tc.nc
     with ExitStack() as ctx:
         keep = ctx.enter_context(tc.tile_pool(name="keep", bufs=1))
-        ring = ctx.enter_context(tc.tile_pool(name="ring", bufs=2))
+        ring = ctx.enter_context(tc.tile_pool(name="ring", bufs=3))
         work = ctx.enter_context(tc.tile_pool(name="work", bufs=3))
         psum = ctx.enter_context(tc.psum_pool(name="psum", bufs=1))
 
@@ -109,8 +109,8 @@ def tile_picked_mixinhopggtan_none_po_kernel(
         sig = [keep.tile([P, SIG_W if t in N1_ON_VECTOR else H_W], F32, name="sig%d" % t) for t in range(PACK)]
         hwin = [keep.tile([P, 2048 if t == 3 else H_W], F32, name="hwin%d" % t) for t in range(PACK)]
         for t in range(PACK):
-            nc.gpsimd.memset(sig[t][:, S:], 0.0)
-            nc.gpsimd.memset(hwin[t][:, S:], 0.0)
+            nc.vector.memset(sig[t][:, S:], 0.0)
+            nc.vector.memset(hwin[t][:, S:], 0.0)
         ident = keep.tile([P, P], F32, name="ident")
         make_identity(nc, ident[:])
 

@@ -3,7 +3,7 @@ from contextlib import ExitStack
 import concourse.mybir as mybir
 from concourse.masks import make_identity
 
-K, T, S, N, H = 512, 2048, 512, 512, 512
+T, S, N = 2048, 512, 512
 FLOPS = 3 * 2 * 512 * 512 * 512
 
 F32 = mybir.dt.float32
@@ -18,18 +18,25 @@ ALU = mybir.AluOpType
 ACT = mybir.ActivationFunctionType
 
 P = 128
-PACK = 4
+PLANES = 4
+LAST = PLANES - 1
+MEMBERS = 4
+QUADRANTS = 4
+PER_COLUMN = 16
+LINE = 4
 HALF = S // 2
-SIG_W = 704
-H_W = 544
+
+WINDOW = S + 32
+WINDOW_WHOLE_LIST = S + 192
+WINDOW_NEGATING = 4 * S
+
 Z_PIECES = (256, 128, 128)
 CHUNKS = (64, 128, 128, 128, 64)
 LAG = 2
-N1_ON_VECTOR = (0,)
-N2_ON_VECTOR = ((0, 3), (1, 3))
-N3_ON_VECTOR = ((0, 2), (0, 3), (1, 3), (2, 3))
-H_ON_SCALAR = (0,)
-CAST_ON_VECTOR = (0,)
+Z_PIECES_SHARED = 2
+CHUNKS_SHARED = 3
+GATHER_BUFFERS = 3
+WORK_BUFFERS = LAG + 1
 
 
 def tile_picked_mixinhopggtan_none_po_kernel(
@@ -39,8 +46,8 @@ def tile_picked_mixinhopggtan_none_po_kernel(
     nc = tc.nc
     with ExitStack() as ctx:
         keep = ctx.enter_context(tc.tile_pool(name="keep", bufs=1))
-        ring = ctx.enter_context(tc.tile_pool(name="ring", bufs=3))
-        work = ctx.enter_context(tc.tile_pool(name="work", bufs=3))
+        ring = ctx.enter_context(tc.tile_pool(name="ring", bufs=GATHER_BUFFERS))
+        work = ctx.enter_context(tc.tile_pool(name="work", bufs=WORK_BUFFERS))
         psum = ctx.enter_context(tc.psum_pool(name="psum", bufs=1))
 
         def gather(on_vector, out, window, offsets, sign=1.0):
@@ -53,39 +60,47 @@ def tile_picked_mixinhopggtan_none_po_kernel(
             else:
                 nc.scalar.activation(out=out, in_=window.indirect(offsets), func=ACT.Copy, scale=sign)
 
-        def load_list(name, src):
-            t = keep.tile(list(src.shape), U16, name=name)
-            nc.sync.dma_start(out=t[:], in_=src)
-            return t
+        def entries(list_tile, first, count):
+            return list_tile[:, first // PER_COLUMN : (first + count) // PER_COLUMN]
 
-        def load_scale_rows(dst, src, queues):
-            for q in range(4):
-                queues[q].dma_start(
+        def load_list(name, src):
+            list_tile = keep.tile(list(src.shape), U16, name=name)
+            nc.sync.dma_start(out=list_tile[:], in_=src)
+            return list_tile
+
+        def load_scale_rows(dst, src):
+            for q in range(QUADRANTS):
+                nc.sync.dma_start(
                     out=dst[32 * q : 32 * q + 4, :].bitcast(I32), in_=src[0, 4 * q : 4 * q + 4, :].bitcast(I32)
                 )
 
-        def deal_words(name, raw, eng):
-            t = keep.tile([P, PACK, P, 2], U8, name=name, align_bytes=64)
-            eng.tensor_copy(out=t[:], in_=raw.rearrange("p (m t b) -> p t m b", t=PACK, b=2))
-            return t
+        def deal_words(name, raw):
+            dealt = keep.tile([P, PLANES, P, 2], U8, name=name, align_bytes=64)
+            nc.vector.tensor_copy(out=dealt[:], in_=raw.rearrange("p (m t b) -> p t m b", t=PLANES, b=2))
+            return dealt
 
         def deal_scales(name, raw):
-            t = keep.tile([P, PACK, P], U8, name=name, align_bytes=64)
-            nc.vector.tensor_copy(out=t[:], in_=raw.rearrange("p (m t) -> p t m", t=PACK))
-            return t
+            dealt = keep.tile([P, PLANES, P], U8, name=name, align_bytes=64)
+            nc.vector.tensor_copy(out=dealt[:], in_=raw.rearrange("p (m t) -> p t m", t=PLANES))
+            return dealt
 
-        def product(out, w, ws, t, codes, scales, start, stop):
+        def product(out, weight, weight_scales, t, codes, scales, start, stop):
             nc.tensor.matmul_mx(
                 out=out,
-                lhsT=w[:, t].rearrange("p m b -> p (m b)").bitcast(FP4X4),
-                lhsT_scale=ws[:, t, :],
+                lhsT=weight[:, t].rearrange("p m b -> p (m b)").bitcast(FP4X4),
+                lhsT_scale=weight_scales[:, t, :],
                 rhs=codes.bitcast(FP8X4),
                 rhs_scale=scales,
                 start=start,
                 stop=stop,
             )
 
-        on_sync = [nc.sync] * 4
+        def by_planes(ap):
+            return ap.rearrange("p t (c i) -> p c t i", i=LINE)
+
+        def by_columns(ap):
+            return ap.rearrange("p (c i) t -> p c t i", i=LINE)
+
         xs = keep.tile([P, T], U8, name="xs")
         nc.vector.memset(xs[:].bitcast(I32), 0)
         ws_raw = keep.tile([P, 2 * N], U8, name="ws_raw")
@@ -94,174 +109,176 @@ def tile_picked_mixinhopggtan_none_po_kernel(
         offs_sb = load_list("offs_sb", offs)
         w1_raw = keep.tile([P, 2 * N], U8, name="w_raw")
         nc.sync.dma_start(out=w1_raw[:].bitcast(I32), in_=w1_words[0].bitcast(I32))
-        load_scale_rows(xs, x_scales, on_sync)
+        load_scale_rows(xs, x_scales)
         xw = keep.tile([P, T], U32, name="xw")
         nc.sync.dma_start(out=xw[:].bitcast(I32), in_=x_words[0].rearrange("p n t -> p (n t)").bitcast(I32))
         w1s_raw = ws_raw[:, N // 2 : N // 2 + N]
-        load_scale_rows(w1s_raw, w1_scales, on_sync)
+        load_scale_rows(w1s_raw, w1_scales)
         two_sb = load_list("two_sb", two)
         n1_sb = load_list("n1_sb", n1)
-        gain = keep.tile([P, PACK], F32, name="gain")
-        nc.gpsimd.dma_start(out=gain[:], in_=gn.rearrange("(p t) o -> p (t o)", t=PACK))
+        gain = keep.tile([P, PLANES], F32, name="gain")
+        nc.scalar.dma_start(out=gain[:], in_=gn.rearrange("(p t) o -> p (t o)", t=PLANES))
         n2_sb = load_list("n2_sb", n2)
         n3_sb = load_list("n3_sb", n3)
 
-        sig = [keep.tile([P, SIG_W if t in N1_ON_VECTOR else H_W], F32, name="sig%d" % t) for t in range(PACK)]
-        hwin = [keep.tile([P, 2048 if t == 3 else H_W], F32, name="hwin%d" % t) for t in range(PACK)]
-        for t in range(PACK):
+        sig = [keep.tile([P, WINDOW_WHOLE_LIST if t == 0 else WINDOW], F32, name="sig%d" % t) for t in range(PLANES)]
+        hwin = [keep.tile([P, WINDOW_NEGATING if t == LAST else WINDOW], F32, name="hwin%d" % t) for t in range(PLANES)]
+        for t in range(PLANES):
             nc.vector.memset(sig[t][:, S:], 0.0)
             nc.vector.memset(hwin[t][:, S:], 0.0)
-        ident = keep.tile([P, P], F32, name="ident")
-        make_identity(nc, ident[:])
 
-        w1 = deal_words("w1", w1_raw[:], nc.vector)
+        w1 = deal_words("w1", w1_raw[:])
         w1s = deal_scales("w1s", w1s_raw)
-        x1s = keep.tile([P, S], U8, name="picked_scales", align_bytes=64)
+        x1s = keep.tile([P, S], U8, name="x1s", align_bytes=64)
         nc.vector.tensor_copy(out=x1s[:], in_=xs[:].indirect(offs_sb[:]))
-        y = [psum.tile([P, S], F32, name="bank%d" % t) for t in range(PACK)]
+        y = [psum.tile([P, S], F32, name="bank%d" % t) for t in range(PLANES)]
         x1w = [keep.tile([P, HALF], U32, name="picked_words%d" % u, align_bytes=64) for u in range(2)]
         for u in range(2):
-            cols = slice(u * HALF, (u + 1) * HALF)
-            nc.vector.tensor_copy(out=x1w[u][:], in_=xw[:].indirect(offs_sb[:, u * 16 : (u + 1) * 16]))
-        for t in range(PACK):
+            nc.vector.tensor_copy(out=x1w[u][:], in_=xw[:].indirect(entries(offs_sb, u * HALF, HALF)))
+        for t in range(PLANES):
             for u in range(2):
                 cols = slice(u * HALF, (u + 1) * HALF)
                 product(y[t][:, cols], w1, w1s, t, x1w[u][:], x1s[:, cols], True, True)
 
-        for t in range(PACK):
+        ident = keep.tile([P, P], F32, name="x1s", align_bytes=64)
+        make_identity(nc, ident[:])
+
+        for t in range(PLANES):
             nc.scalar.activation(out=sig[t][:, :S], in_=y[t][:], func=ACT.Sigmoid)
 
-        st = keep.tile([P, PACK, S], F32, name="st")
-        sg = [keep.tile([P, S], F32, name="sg%d" % t) for t in range(PACK)]
-        for t in range(PACK):
-            gather(t in N1_ON_VECTOR, sg[t][:], sig[t][:], n1_sb[:])
+        st = keep.tile([P, PLANES, S], F32, name="st")
+        sg = [keep.tile([P, S], F32, name="sg%d" % t) for t in range(PLANES)]
+        for t in range(PLANES):
+            gather(t == 0, sg[t][:], sig[t][:], n1_sb[:])
             nc.vector.scalar_tensor_tensor(
                 out=st[:, t, :], in0=y[t][:], scalar=gain[:, t : t + 1], in1=sg[t][:], op0=ALU.mult, op1=ALU.mult
             )
 
         x2w = [keep.tile([P, HALF], U32, name="picked_words%d" % u, align_bytes=64) for u in range(2)]
         for u in range(2):
-            nc.vector.tensor_copy(out=x2w[u][:], in_=xw[:].indirect(two_sb[:, u * 16 : (u + 1) * 16]))
+            nc.vector.tensor_copy(out=x2w[u][:], in_=xw[:].indirect(entries(two_sb, u * HALF, HALF)))
         x2s = keep.tile([P, S], U8, name="x2s", align_bytes=64)
         nc.vector.tensor_copy(out=x2s[:], in_=xs[:].indirect(two_sb[:]))
 
-        w_late = keep.tile([P, 2, 2 * N], U8, name="w_raw")
-        nc.sync.dma_start(out=w_late[:, 0, :].bitcast(I32), in_=w3_words[0].bitcast(I32))
-        load_scale_rows(ws_raw[:, :N], w3_scales, on_sync)
-        nc.sync.dma_start(out=w_late[:, 1, :].bitcast(I32), in_=w2_words[0].bitcast(I32))
-        load_scale_rows(ws_raw[:, N:], w2_scales, on_sync)
-        w3 = deal_words("w3", w_late[:, 0, :], nc.vector)
+        w32_raw = keep.tile([P, 2, 2 * N], U8, name="w_raw")
+        nc.sync.dma_start(out=w32_raw[:, 0, :].bitcast(I32), in_=w3_words[0].bitcast(I32))
+        load_scale_rows(ws_raw[:, :N], w3_scales)
+        nc.sync.dma_start(out=w32_raw[:, 1, :].bitcast(I32), in_=w2_words[0].bitcast(I32))
+        load_scale_rows(ws_raw[:, N:], w2_scales)
+        w3 = deal_words("w3", w32_raw[:, 0, :])
         w3s = deal_scales("w3s", ws_raw[:, :N])
-        w2 = deal_words("w2", w_late[:, 1, :], nc.vector)
+        w2 = deal_words("w2", w32_raw[:, 1, :])
         w2s = deal_scales("w2s", ws_raw[:, N:])
-        h = [psum.tile([P, S], F32, name="h%d" % t) for t in range(PACK)]
+        h = [psum.tile([P, S], F32, name="h%d" % t) for t in range(PLANES)]
         for u in range(2):
             cols = slice(u * HALF, (u + 1) * HALF)
-            for t in range(PACK):
+            for t in range(PLANES):
                 product(h[t][:, cols], w3, w3s, t, x2w[u][:], x2s[:, cols], u == 0, False)
 
-        early = keep.tile([P, PACK * HALF], F32, name="early")
-        late = keep.tile([P, PACK * HALF], F32, name="sg3")
+        looked_up = [keep.tile([P, PLANES * HALF], F32, name=name) for name in ("looked_up", "sg%d" % LAST)]
         c0 = 0
-        for u, w in enumerate(Z_PIECES):
-            cols = slice(c0, c0 + w)
-            st2 = early if c0 < HALF else late
-            st2 = st2[:, PACK * (c0 % HALF) : PACK * (c0 % HALF + w)].rearrange("p (t c) -> p t c", t=PACK)
-            for t in range(PACK):
-                gather((u, t) in N2_ON_VECTOR, st2[:, t, :], st[:, t, :], n2_sb[:, c0 // 16 : (c0 + w) // 16])
-            zb = keep.tile([P, w, PACK], BF16, name="zb%d" % u, align_bytes=64)
+        for piece, width in enumerate(Z_PIECES):
+            cols = slice(c0, c0 + width)
+            at = PLANES * (c0 % HALF)
+            st_n2 = looked_up[c0 // HALF][:, at : at + PLANES * width].rearrange("p (t c) -> p t c", t=PLANES)
+            for t in range(PLANES):
+                on_vector = t == LAST and piece < Z_PIECES_SHARED
+                gather(on_vector, st_n2[:, t, :], st[:, t, :], entries(n2_sb, c0, width))
+            zb = keep.tile([P, width, PLANES], BF16, name="zb%d" % piece, align_bytes=64)
             nc.vector.tensor_tensor(
-                out=zb[:].rearrange("p (c i) t -> p c t i", i=4),
-                in0=st[:, :, cols].rearrange("p t (c i) -> p c t i", i=4),
-                in1=st2.rearrange("p t (c i) -> p c t i", i=4),
-                op=ALU.subtract,
+                out=by_columns(zb[:]), in0=by_planes(st[:, :, cols]), in1=by_planes(st_n2), op=ALU.subtract
             )
-            zw = keep.tile([P, w], U32, name="zw%d" % u, align_bytes=64)
-            zs = keep.tile([P, w], U8, name="zs%d" % u, align_bytes=64)
+            zw = keep.tile([P, width], U32, name="zw%d" % piece, align_bytes=64)
+            zs = keep.tile([P, width], U8, name="zs%d" % piece, align_bytes=64)
             nc.vector.quantize_mx(out=zw[:].bitcast(FP8X4), scales=zs[:], in_=zb[:].rearrange("p c t -> p (c t)"))
-            for t in range(PACK):
-                product(h[t][:, cols], w2, w2s, t, zw[:], zs[:], False, u == len(Z_PIECES) - 1)
-            c0 = c0 + w
+            for t in range(PLANES):
+                product(h[t][:, cols], w2, w2s, t, zw[:], zs[:], False, piece == len(Z_PIECES) - 1)
+            c0 = c0 + width
 
-        for t in range(PACK):
-            if t in H_ON_SCALAR:
+        for t in range(PLANES):
+            if t == 0:
                 nc.scalar.copy(out=hwin[t][:, :S], in_=h[t][:])
             else:
                 nc.vector.tensor_copy(out=hwin[t][:, :S], in_=h[t][:])
 
-        ow = keep.tile([P, S], U32, name="ow", align_bytes=64)
-        osc = keep.tile([P, S], U8, name="osc", align_bytes=64)
-        out_rows = out_0.rearrange("(p t) c -> p t c", t=PACK)
+        out_codes = keep.tile([P, S], U32, name="out_codes", align_bytes=64)
+        out_scales = keep.tile([P, S], U8, name="out_scales", align_bytes=64)
+        out_rows = out_0.rearrange("(p t) c -> p t c", t=PLANES)
         out_words = out_1[0].rearrange("p c r -> p (c r)").bitcast(I32)
 
-        def finish(c, c0, w, factor, th):
-            cols = slice(c0, c0 + w)
-            o = work.tile([P, PACK, w], F32, name="o")
-            nc.vector.tensor_tensor(out=o[:], in0=factor[:], in1=th[:], op=ALU.mult)
-            nc.sync.dma_start(out=out_rows[:, :, cols], in_=o[:])
-            ob = work.tile([P, w, PACK], BF16, name="ob", align_bytes=64)
-            dst = ob[:].rearrange("p (c i) t -> p c t i", i=4)
-            src = o[:].rearrange("p t (c i) -> p c t i", i=4)
-            if c in CAST_ON_VECTOR:
-                nc.vector.tensor_copy(out=dst, in_=src)
+        def finish(chunk, cols, width, factor, th):
+            result = work.tile([P, PLANES, width], F32, name="result")
+            nc.vector.tensor_tensor(out=result[:], in0=factor[:], in1=th[:], op=ALU.mult)
+            nc.sync.dma_start(out=out_rows[:, :, cols], in_=result[:])
+            rounded = work.tile([P, width, PLANES], BF16, name="rounded", align_bytes=64)
+            if chunk == 0:
+                nc.vector.tensor_copy(out=by_columns(rounded[:]), in_=by_planes(result[:]))
             else:
-                nc.scalar.copy(out=dst, in_=src)
+                nc.scalar.copy(out=by_columns(rounded[:]), in_=by_planes(result[:]))
             nc.vector.quantize_mx(
-                out=ow[:, cols].bitcast(FP8X4), scales=osc[:, cols], in_=ob[:].rearrange("p c t -> p (c t)")
+                out=out_codes[:, cols].bitcast(FP8X4),
+                scales=out_scales[:, cols],
+                in_=rounded[:].rearrange("p c t -> p (c t)"),
             )
-            nc.sync.dma_start(out=out_words[:, cols], in_=ow[:, cols].bitcast(I32))
+            nc.sync.dma_start(out=out_words[:, cols], in_=out_codes[:, cols].bitcast(I32))
 
         c0 = 0
         pending = []
-        for c, w in enumerate(CHUNKS):
-            cols = slice(c0, c0 + w)
-            on_tensor = w == P
+        for chunk, width in enumerate(CHUNKS):
+            cols = slice(c0, c0 + width)
+            on_tensor = width == P
             sign = -1.0 if on_tensor else 1.0
             inner_op, factor_op = (ALU.max, ALU.min) if on_tensor else (ALU.min, ALU.max)
-            mb = ring.tile([P, PACK, 4 * w], F32, name="mb")
-            for t in range(PACK):
-                gather((c, t) in N3_ON_VECTOR, mb[:, t, :], hwin[t][:], n3_sb[:, c0 // 4 : (c0 + w) // 4], sign)
-            members = mb[:].rearrange("p t (j m) -> p (t j) m", m=4)
-            inner2 = work.tile([P, PACK * w, 2], F32, name="inner2")
-            factor2 = work.tile([P, PACK * w, 2], F32, name="factor2")
-            factor = work.tile([P, PACK, w], F32, name="factor")
-            spent = mb[:, 0, :].rearrange("p (t j) -> p t j", t=PACK)
-            inner = spent if on_tensor else work.tile([P, PACK, w], F32, name="inner")[:]
-            steps = [(inner2, inner, inner_op), (factor2, factor[:], factor_op)]
+            mb = ring.tile([P, PLANES, MEMBERS * width], F32, name="mb")
+            for t in range(PLANES):
+                on_vector = (t == LAST and chunk < CHUNKS_SHARED) or (t == LAST - 1 and chunk == 0)
+                gather(on_vector, mb[:, t, :], hwin[t][:], entries(n3_sb, MEMBERS * c0, MEMBERS * width), sign)
+            members = mb[:].rearrange("p t (j m) -> p (t j) m", m=MEMBERS)
+            inner_pairs = work.tile([P, PLANES * width, 2], F32, name="inner_pairs")
+            factor_pairs = work.tile([P, PLANES * width, 2], F32, name="factor_pairs")
+            factor = work.tile([P, PLANES, width], F32, name="factor")
+            spent = mb[:, 0, :].rearrange("p (t j) -> p t j", t=PLANES)
+            inner = spent if on_tensor else work.tile([P, PLANES, width], F32, name="inner")[:]
+            steps = [(inner_pairs, inner, inner_op), (factor_pairs, factor[:], factor_op)]
             if on_tensor:
                 steps = steps[::-1]
-            for pairs, whole, op in steps:
+            for pairs, extreme, op in steps:
                 nc.vector.tensor_tensor(out=pairs[:], in0=members[:, :, 0:2], in1=members[:, :, 2:4], op=op)
-            for pairs, whole, op in steps:
+            for pairs, extreme, op in steps:
                 nc.vector.tensor_tensor(
-                    out=whole.rearrange("p t j -> p (t j)"), in0=pairs[:, :, 0], in1=pairs[:, :, 1], op=op
+                    out=extreme.rearrange("p t j -> p (t j)"), in0=pairs[:, :, 0], in1=pairs[:, :, 1], op=op
                 )
             if on_tensor:
-                d_t = psum.tile([P, PACK, P], F32, name="bank%d" % (c % 2))
-                for t in range(PACK):
-                    nc.tensor.matmul(d_t[:, t, :], hwin[t][:, cols], ident[:], start=True, stop=False, is_transpose=True)
-                    nc.tensor.matmul(d_t[:, t, :], inner[:, t, :], ident[:], start=False, stop=True, is_transpose=True)
-                th_t = work.tile([P, PACK, P], F32, name="th_t")
-                nc.scalar.activation(out=th_t[:], in_=d_t[:], func=ACT.Tanh, scale=-1.0)
-                th = psum.tile([P, PACK, P], F32, name="bank%d" % (2 + c % 2))
-                for t in range(PACK):
+                diff_t = psum.tile([P, PLANES, P], F32, name="bank%d" % (chunk % 2))
+                for t in range(PLANES):
+                    nc.tensor.matmul(
+                        diff_t[:, t, :], hwin[t][:, cols], ident[:], start=True, stop=False, is_transpose=True
+                    )
+                    nc.tensor.matmul(
+                        diff_t[:, t, :], inner[:, t, :], ident[:], start=False, stop=True, is_transpose=True
+                    )
+                th_t = work.tile([P, PLANES, P], F32, name="th_t")
+                nc.scalar.activation(out=th_t[:], in_=diff_t[:], func=ACT.Tanh, scale=-1.0)
+                th = psum.tile([P, PLANES, P], F32, name="bank%d" % (2 + chunk % 2))
+                for t in range(PLANES):
                     nc.tensor.transpose(th[:, t, :], th_t[:, t, :], ident[:])
             else:
-                d = spent
-                for t in range(PACK):
-                    nc.vector.tensor_tensor(out=d[:, t, :], in0=h[t][:, cols], in1=inner[:, t, :], op=ALU.subtract)
-                th = work.tile([P, PACK, w], F32, name="th")
-                nc.scalar.activation(out=th[:], in_=d, func=ACT.Tanh)
-            pending.append((c, c0, w, factor, th))
-            if len(pending) > LAG:
-                finish(*pending[0])
-                pending = pending[1:]
-            c0 = c0 + w
-        for rest in pending:
-            finish(*rest)
+                for t in range(PLANES):
+                    nc.vector.tensor_tensor(
+                        out=spent[:, t, :], in0=h[t][:, cols], in1=inner[:, t, :], op=ALU.subtract
+                    )
+                th = work.tile([P, PLANES, width], F32, name="th")
+                nc.scalar.activation(out=th[:], in_=spent, func=ACT.Tanh)
+            pending.append((chunk, cols, width, factor, th))
+            for waiting in pending[:-LAG]:
+                finish(*waiting)
+            pending = pending[-LAG:]
+            c0 = c0 + width
+        for waiting in pending:
+            finish(*waiting)
 
-        for q in range(4):
-            eng = nc.scalar if q % 2 == 0 else nc.sync
-            eng.dma_start(
-                out=out_2[0, 4 * q : 4 * q + 4, :].bitcast(I32), in_=osc[32 * q : 32 * q + 4, :].bitcast(I32)
+        for q in range(QUADRANTS):
+            queue = nc.scalar if q % 2 == 0 else nc.sync
+            queue.dma_start(
+                out=out_2[0, 4 * q : 4 * q + 4, :].bitcast(I32), in_=out_scales[32 * q : 32 * q + 4, :].bitcast(I32)
             )

@@ -116,16 +116,18 @@ def tile_picked_mixinhopggtan_none_po_kernel(
         load_scale_rows(w1s_raw, w1_scales)
         two_sb = load_list("two_sb", two)
         n1_sb = load_list("n1_sb", n1)
-        gain = keep.tile([P, PLANES], F32, name="gain")
-        nc.scalar.dma_start(out=gain[:], in_=gn.rearrange("(p t) o -> p (t o)", t=PLANES))
         n2_sb = load_list("n2_sb", n2)
         n3_sb = load_list("n3_sb", n3)
+        gain = keep.tile([P, PLANES], F32, name="gain")
+        nc.sync.dma_start(out=gain[:], in_=gn.rearrange("(p t) o -> p (t o)", t=PLANES))
 
         sig = [keep.tile([P, WINDOW_WHOLE_LIST if t == 0 else WINDOW], F32, name="sig%d" % t) for t in range(PLANES)]
         hwin = [keep.tile([P, WINDOW_NEGATING if t == LAST else WINDOW], F32, name="hwin%d" % t) for t in range(PLANES)]
         for t in range(PLANES):
             nc.vector.memset(sig[t][:, S:], 0.0)
             nc.vector.memset(hwin[t][:, S:], 0.0)
+        ident = keep.tile([P, P], F32, name="ident")
+        make_identity(nc, ident[:])
 
         w1 = deal_words("w1", w1_raw[:])
         w1s = deal_scales("w1s", w1s_raw)
@@ -139,9 +141,6 @@ def tile_picked_mixinhopggtan_none_po_kernel(
             for u in range(2):
                 cols = slice(u * HALF, (u + 1) * HALF)
                 product(y[t][:, cols], w1, w1s, t, x1w[u][:], x1s[:, cols], True, True)
-
-        ident = keep.tile([P, P], F32, name="x1s", align_bytes=64)
-        make_identity(nc, ident[:])
 
         for t in range(PLANES):
             nc.scalar.activation(out=sig[t][:, :S], in_=y[t][:], func=ACT.Sigmoid)

from contextlib import ExitStack

import concourse.mybir as mybir
from concourse.masks import make_identity

T, S, N = 2048, 512, 512
FLOPS = 3 * 2 * 512 * 512 * 512

F32 = mybir.dt.float32
BF16 = mybir.dt.bfloat16
I32 = mybir.dt.int32
U32 = mybir.dt.uint32
U16 = mybir.dt.uint16
U8 = mybir.dt.uint8
FP8X4 = mybir.dt.float8_e4m3fn_x4
FP4X4 = mybir.dt.float4_e2m1fn_x4
ALU = mybir.AluOpType
ACT = mybir.ActivationFunctionType

P = 128
PLANES = 4
LAST = PLANES - 1
MEMBERS = 4
QUADRANTS = 4
PER_COLUMN = 16
LINE = 4
HALF = S // 2

WINDOW = S + 32
WINDOW_WHOLE_LIST = S + 192
WINDOW_NEGATING = 4 * S

Z_PIECES = (256, 128, 128)
CHUNKS = (64, 128, 128, 128, 64)
LAG = 2
Z_PIECES_SHARED = 2
CHUNKS_SHARED = 3
GATHER_BUFFERS = 3
WORK_BUFFERS = LAG + 1


def tile_picked_mixinhopggtan_none_po_kernel(
    tc, x_words, x_scales, w1_words, w1_scales, gn, w2_words, w2_scales, w3_words, w3_scales,
    offs, n1, n2, two, n3, out_0, out_1, out_2,
):
    nc = tc.nc
    with ExitStack() as ctx:
        keep = ctx.enter_context(tc.tile_pool(name="keep", bufs=1))
        ring = ctx.enter_context(tc.tile_pool(name="ring", bufs=GATHER_BUFFERS))
        work = ctx.enter_context(tc.tile_pool(name="work", bufs=WORK_BUFFERS))
        psum = ctx.enter_context(tc.psum_pool(name="psum", bufs=1))

        def gather(on_vector, out, window, offsets, sign=1.0):
            if on_vector and sign < 0:
                nc.vector.tensor_scalar(
                    out=out, in0=window.indirect(offsets), scalar1=sign, scalar2=0.0, op0=ALU.mult, op1=ALU.add
                )
            elif on_vector:
                nc.vector.tensor_copy(out=out, in_=window.indirect(offsets))
            else:
                nc.scalar.activation(out=out, in_=window.indirect(offsets), func=ACT.Copy, scale=sign)

        def entries(list_tile, first, count):
            return list_tile[:, first // PER_COLUMN : (first + count) // PER_COLUMN]

        def load_list(name, src):
            list_tile = keep.tile(list(src.shape), U16, name=name)
            nc.sync.dma_start(out=list_tile[:], in_=src)
            return list_tile

        def load_scale_rows(dst, src):
            for q in range(QUADRANTS):
                nc.sync.dma_start(
                    out=dst[32 * q : 32 * q + 4, :].bitcast(I32), in_=src[0, 4 * q : 4 * q + 4, :].bitcast(I32)
                )

        def deal_words(name, raw):
            dealt = keep.tile([P, PLANES, P, 2], U8, name=name, align_bytes=64)
            nc.vector.tensor_copy(out=dealt[:], in_=raw.rearrange("p (m t b) -> p t m b", t=PLANES, b=2))
            return dealt

        def deal_scales(name, raw):
            dealt = keep.tile([P, PLANES, P], U8, name=name, align_bytes=64)
            nc.vector.tensor_copy(out=dealt[:], in_=raw.rearrange("p (m t) -> p t m", t=PLANES))
            return dealt

        def product(out, weight, weight_scales, t, codes, scales, start, stop):
            nc.tensor.matmul_mx(
                out=out,
                lhsT=weight[:, t].rearrange("p m b -> p (m b)").bitcast(FP4X4),
                lhsT_scale=weight_scales[:, t, :],
                rhs=codes.bitcast(FP8X4),
                rhs_scale=scales,
                start=start,
                stop=stop,
            )

        def by_planes(ap):
            return ap.rearrange("p t (c i) -> p c t i", i=LINE)

        def by_columns(ap):
            return ap.rearrange("p (c i) t -> p c t i", i=LINE)

        xs = keep.tile([P, T], U8, name="xs")
        nc.vector.memset(xs[:].bitcast(I32), 0)
        ws_raw = keep.tile([P, 2 * N], U8, name="ws_raw")
        nc.vector.memset(ws_raw[:].bitcast(I32), 0)

        offs_sb = load_list("offs_sb", offs)
        w1_raw = keep.tile([P, 2 * N], U8, name="w_raw")
        nc.sync.dma_start(out=w1_raw[:].bitcast(I32), in_=w1_words[0].bitcast(I32))
        load_scale_rows(xs, x_scales)
        xw = keep.tile([P, T], U32, name="xw")
        nc.sync.dma_start(out=xw[:].bitcast(I32), in_=x_words[0].rearrange("p n t -> p (n t)").bitcast(I32))
        w1s_raw = ws_raw[:, N // 2 : N // 2 + N]
        load_scale_rows(w1s_raw, w1_scales)
        two_sb = load_list("two_sb", two)
        n1_sb = load_list("n1_sb", n1)
        n2_sb = load_list("n2_sb", n2)
        n3_sb = load_list("n3_sb", n3)
        gain = keep.tile([P, PLANES], F32, name="gain")
        nc.sync.dma_start(out=gain[:], in_=gn.rearrange("(p t) o -> p (t o)", t=PLANES))

        sig = [keep.tile([P, WINDOW_WHOLE_LIST if t == 0 else WINDOW], F32, name="sig%d" % t) for t in range(PLANES)]
        hwin = [keep.tile([P, WINDOW_NEGATING if t == LAST else WINDOW], F32, name="hwin%d" % t) for t in range(PLANES)]
        for t in range(PLANES):
            nc.vector.memset(sig[t][:, S:], 0.0)
            nc.vector.memset(hwin[t][:, S:], 0.0)
        ident = keep.tile([P, P], F32, name="ident")
        make_identity(nc, ident[:])

        w1 = deal_words("w1", w1_raw[:])
        w1s = deal_scales("w1s", w1s_raw)
        x1s = keep.tile([P, S], U8, name="x1s", align_bytes=64)
        nc.vector.tensor_copy(out=x1s[:], in_=xs[:].indirect(offs_sb[:]))
        y = [psum.tile([P, S], F32, name="bank%d" % t) for t in range(PLANES)]
        x1w = [keep.tile([P, HALF], U32, name="picked_words%d" % u, align_bytes=64) for u in range(2)]
        for u in range(2):
            nc.vector.tensor_copy(out=x1w[u][:], in_=xw[:].indirect(entries(offs_sb, u * HALF, HALF)))
        for t in range(PLANES):
            for u in range(2):
                cols = slice(u * HALF, (u + 1) * HALF)
                product(y[t][:, cols], w1, w1s, t, x1w[u][:], x1s[:, cols], True, True)

        for t in range(PLANES):
            nc.scalar.activation(out=sig[t][:, :S], in_=y[t][:], func=ACT.Sigmoid)

        st = keep.tile([P, PLANES, S], F32, name="st")
        sg = [keep.tile([P, S], F32, name="sg%d" % t) for t in range(PLANES)]
        for t in range(PLANES):
            gather(t == 0, sg[t][:], sig[t][:], n1_sb[:])
            nc.vector.scalar_tensor_tensor(
                out=st[:, t, :], in0=y[t][:], scalar=gain[:, t : t + 1], in1=sg[t][:], op0=ALU.mult, op1=ALU.mult
            )

        x2w = [keep.tile([P, HALF], U32, name="picked_words%d" % u, align_bytes=64) for u in range(2)]
        for u in range(2):
            nc.vector.tensor_copy(out=x2w[u][:], in_=xw[:].indirect(entries(two_sb, u * HALF, HALF)))
        x2s = keep.tile([P, S], U8, name="x2s", align_bytes=64)
        nc.vector.tensor_copy(out=x2s[:], in_=xs[:].indirect(two_sb[:]))

        w32_raw = keep.tile([P, 2, 2 * N], U8, name="w_raw")
        nc.sync.dma_start(out=w32_raw[:, 0, :].bitcast(I32), in_=w3_words[0].bitcast(I32))
        load_scale_rows(ws_raw[:, :N], w3_scales)
        nc.sync.dma_start(out=w32_raw[:, 1, :].bitcast(I32), in_=w2_words[0].bitcast(I32))
        load_scale_rows(ws_raw[:, N:], w2_scales)
        w3 = deal_words("w3", w32_raw[:, 0, :])
        w3s = deal_scales("w3s", ws_raw[:, :N])
        w2 = deal_words("w2", w32_raw[:, 1, :])
        w2s = deal_scales("w2s", ws_raw[:, N:])
        h = [psum.tile([P, S], F32, name="h%d" % t) for t in range(PLANES)]
        for u in range(2):
            cols = slice(u * HALF, (u + 1) * HALF)
            for t in range(PLANES):
                product(h[t][:, cols], w3, w3s, t, x2w[u][:], x2s[:, cols], u == 0, False)

        looked_up = [keep.tile([P, PLANES * HALF], F32, name=name) for name in ("looked_up", "sg%d" % LAST)]
        c0 = 0
        for piece, width in enumerate(Z_PIECES):
            cols = slice(c0, c0 + width)
            at = PLANES * (c0 % HALF)
            st_n2 = looked_up[c0 // HALF][:, at : at + PLANES * width].rearrange("p (t c) -> p t c", t=PLANES)
            for t in range(PLANES):
                on_vector = t == LAST and piece < Z_PIECES_SHARED
                gather(on_vector, st_n2[:, t, :], st[:, t, :], entries(n2_sb, c0, width))
            zb = keep.tile([P, width, PLANES], BF16, name="zb%d" % piece, align_bytes=64)
            nc.vector.tensor_tensor(
                out=by_columns(zb[:]), in0=by_planes(st[:, :, cols]), in1=by_planes(st_n2), op=ALU.subtract
            )
            zw = keep.tile([P, width], U32, name="zw%d" % piece, align_bytes=64)
            zs = keep.tile([P, width], U8, name="zs%d" % piece, align_bytes=64)
            nc.vector.quantize_mx(out=zw[:].bitcast(FP8X4), scales=zs[:], in_=zb[:].rearrange("p c t -> p (c t)"))
            for t in range(PLANES):
                product(h[t][:, cols], w2, w2s, t, zw[:], zs[:], False, piece == len(Z_PIECES) - 1)
            c0 = c0 + width

        for t in range(PLANES):
            if t == 0:
                nc.scalar.copy(out=hwin[t][:, :S], in_=h[t][:])
            else:
                nc.vector.tensor_copy(out=hwin[t][:, :S], in_=h[t][:])

        out_codes = keep.tile([P, S], U32, name="out_codes", align_bytes=64)
        out_scales = keep.tile([P, S], U8, name="out_scales", align_bytes=64)
        out_rows = out_0.rearrange("(p t) c -> p t c", t=PLANES)
        out_words = out_1[0].rearrange("p c r -> p (c r)").bitcast(I32)

        def finish(chunk, cols, width, factor, th):
            result = work.tile([P, PLANES, width], F32, name="result")
            nc.vector.tensor_tensor(out=result[:], in0=factor[:], in1=th[:], op=ALU.mult)
            nc.sync.dma_start(out=out_rows[:, :, cols], in_=result[:])
            rounded = work.tile([P, width, PLANES], BF16, name="rounded", align_bytes=64)
            if chunk == 0:
                nc.vector.tensor_copy(out=by_columns(rounded[:]), in_=by_planes(result[:]))
            else:
                nc.scalar.copy(out=by_columns(rounded[:]), in_=by_planes(result[:]))
            nc.vector.quantize_mx(
                out=out_codes[:, cols].bitcast(FP8X4),
                scales=out_scales[:, cols],
                in_=rounded[:].rearrange("p c t -> p (c t)"),
            )
            nc.sync.dma_start(out=out_words[:, cols], in_=out_codes[:, cols].bitcast(I32))

        c0 = 0
        pending = []
        for chunk, width in enumerate(CHUNKS):
            cols = slice(c0, c0 + width)
            on_tensor = width == P
            sign = -1.0 if on_tensor else 1.0
            inner_op, factor_op = (ALU.max, ALU.min) if on_tensor else (ALU.min, ALU.max)
            mb = ring.tile([P, PLANES, MEMBERS * width], F32, name="mb")
            for t in range(PLANES):
                on_vector = (t == LAST and chunk < CHUNKS_SHARED) or (t == LAST - 1 and chunk == 0)
                gather(on_vector, mb[:, t, :], hwin[t][:], entries(n3_sb, MEMBERS * c0, MEMBERS * width), sign)
            members = mb[:].rearrange("p t (j m) -> p (t j) m", m=MEMBERS)
            inner_pairs = work.tile([P, PLANES * width, 2], F32, name="inner_pairs")
            factor_pairs = work.tile([P, PLANES * width, 2], F32, name="factor_pairs")
            factor = work.tile([P, PLANES, width], F32, name="factor")
            spent = mb[:, 0, :].rearrange("p (t j) -> p t j", t=PLANES)
            inner = spent if on_tensor else work.tile([P, PLANES, width], F32, name="inner")[:]
            steps = [(inner_pairs, inner, inner_op), (factor_pairs, factor[:], factor_op)]
            if on_tensor:
                steps = steps[::-1]
            for pairs, extreme, op in steps:
                nc.vector.tensor_tensor(out=pairs[:], in0=members[:, :, 0:2], in1=members[:, :, 2:4], op=op)
            for pairs, extreme, op in steps:
                nc.vector.tensor_tensor(
                    out=extreme.rearrange("p t j -> p (t j)"), in0=pairs[:, :, 0], in1=pairs[:, :, 1], op=op
                )
            if on_tensor:
                diff_t = psum.tile([P, PLANES, P], F32, name="bank%d" % (chunk % 2))
                for t in range(PLANES):
                    nc.tensor.matmul(
                        diff_t[:, t, :], hwin[t][:, cols], ident[:], start=True, stop=False, is_transpose=True
                    )
                    nc.tensor.matmul(
                        diff_t[:, t, :], inner[:, t, :], ident[:], start=False, stop=True, is_transpose=True
                    )
                th_t = work.tile([P, PLANES, P], F32, name="th_t")
                nc.scalar.activation(out=th_t[:], in_=diff_t[:], func=ACT.Tanh, scale=-1.0)
                th = psum.tile([P, PLANES, P], F32, name="bank%d" % (2 + chunk % 2))
                for t in range(PLANES):
                    nc.tensor.transpose(th[:, t, :], th_t[:, t, :], ident[:])
            else:
                for t in range(PLANES):
                    nc.vector.tensor_tensor(
                        out=spent[:, t, :], in0=h[t][:, cols], in1=inner[:, t, :], op=ALU.subtract
                    )
                th = work.tile([P, PLANES, width], F32, name="th")
                nc.scalar.activation(out=th[:], in_=spent, func=ACT.Tanh)
            pending.append((chunk, cols, width, factor, th))
            for waiting in pending[:-LAG]:
                finish(*waiting)
            pending = pending[-LAG:]
            c0 = c0 + width
        for waiting in pending:
            finish(*waiting)

        for q in range(QUADRANTS):
            queue = nc.scalar if q % 2 == 0 else nc.sync
            queue.dma_start(
                out=out_2[0, 4 * q : 4 * q + 4, :].bitcast(I32), in_=out_scales[32 * q : 32 * q + 4, :].bitcast(I32)
            )
